import numpy as np
import ml_dtypes


def mxq(x, axis, fmt="e4m3"):
    dtype, down = {"e4m3": (ml_dtypes.float8_e4m3fn, 7), "e5m2": (ml_dtypes.float8_e5m2, 14)}[fmt]
    v = np.moveaxis(np.asarray(x, np.float32).astype(ml_dtypes.bfloat16).astype(np.float64), axis, -1)
    blocks = v.reshape(v.shape[:-1] + (-1, 32))
    amax = np.abs(blocks).max(-1, keepdims=True)
    byte = np.maximum(np.where(amax > 0, np.frexp(amax)[1] - 1 + 127, 0) - down, 1)
    scale = np.exp2(byte - 127.0)
    codes = (blocks / scale).astype(np.float32).astype(dtype).astype(np.float64)
    return np.moveaxis((codes * scale).reshape(v.shape), -1, axis)


WIDE = False


def mx_kscale(k):
    if not WIDE:
        return np.ones(k)
    levels = np.array([10, -10, 5, -5, 0])
    if k % 512:
        return np.exp2(np.random.permutation(np.resize(levels, k // 32))).repeat(32)
    a = np.empty((k // 512, 16))
    for p in range(k // 512):
        a[p, :8] = np.random.permutation(np.resize(levels, 8))
        for g in range(8):
            far = levels[np.abs(levels - a[p, g]) >= 10]
            a[p, g + 8] = far[np.random.randint(len(far))]
    return np.exp2(a.ravel()).repeat(32)


def f64(x):
    return np.asarray(x).astype(np.float64)


def striped(idx):
    return np.tile(idx.reshape(-1, 16).T, (8, 1)).astype(np.uint16)


def unstriped(offs):
    return offs[:16].T.reshape(-1).astype(np.int64)


K, T, S, V, N = 512, 1024, 512, 512, 1024


def setup_inputs():
    n = np.random.standard_normal
    s = mx_kscale(K)[:, None]
    return {
        "xT": (n((K, T)) * s).astype(np.float32),
        "w": (n((K, N)) / np.sqrt(K) / s).astype(np.float32),
        "b": (0.3 * n((V, 1))).astype(np.float32),
        "offs": striped(np.random.permutation(T)[:S]),
        "pos1": striped(np.random.permutation(N)[:V]),
    }


def reference(xT, w, b, offs, pos1):
    y = mxq(f64(w)[:, unstriped(pos1)], 0, "e4m3").T @ mxq(f64(xT)[:, unstriped(offs)], 0, "e4m3")
    return y + f64(b)

@@ -1,0 +1,134 @@
+from contextlib import ExitStack
+
+import concourse.mybir as mybir
+from concourse.masks import make_identity
+
+F32 = mybir.dt.float32
+BF16 = mybir.dt.bfloat16
+U16 = mybir.dt.uint16
+U32 = mybir.dt.uint32
+U8 = mybir.dt.uint8
+FP8X4 = mybir.dt.float8_e4m3fn_x4
+COPY = mybir.ActivationFunctionType.Copy
+IDENTITY = mybir.ActivationFunctionType.Identity
+ADD = mybir.AluOpType.add
+
+P = 128
+PACK = 4
+K, T, S, V, N = 512, 1024, 512, 512, 1024
+CHUNK = 128
+CHUNKS = V // CHUNK
+FLOPS = 2 * K * S * V
+
+
+def tile_picked_cross_bias_l_kernel(tc, xT, w, b, offs, pos1, out):
+    nc = tc.nc
+    with ExitStack() as ctx:
+        lists = ctx.enter_context(tc.tile_pool(name="lists", bufs=1))
+        keep = ctx.enter_context(tc.tile_pool(name="keep", bufs=1))
+        psum = ctx.enter_context(tc.psum_pool(name="psum", bufs=1))
+
+        offs_t = lists.tile([P, S // 16], U16, name="offs_t")
+        pos1_t = lists.tile([P, V // 16], U16, name="pos1_t")
+
+        x_rows = xT.rearrange("(p t) n -> p t n", t=PACK)
+        w_rows = w.rearrange("(p t) n -> p t n", t=PACK)
+        x_raw = [keep.tile([P, T], F32, name=f"x_raw{t}") for t in range(PACK)]
+        w_raw = [keep.tile([P, N], F32, name=f"w_raw{t}") for t in range(PACK)]
+
+        nc.sync.dma_start(out=offs_t[:], in_=offs)
+        nc.sync.dma_start(out=x_raw[0][:], in_=x_rows[:, 0, :])
+        nc.sync.dma_start(out=x_raw[1][:], in_=x_rows[:, 1, :])
+        nc.sync.dma_start(out=pos1_t[:], in_=pos1)
+        nc.sync.dma_start(out=w_raw[0][:], in_=w_rows[:, 0, :])
+        nc.sync.dma_start(out=x_raw[2][:], in_=x_rows[:, 2, :])
+        nc.sync.dma_start(out=x_raw[3][:], in_=x_rows[:, 3, :])
+        for t in range(1, PACK):
+            nc.sync.dma_start(out=w_raw[t][:], in_=w_rows[:, t, :])
+
+        b_rows = keep.tile([P, P], F32, name="b_rows")
+        nc.vector.memset(b_rows[:], 0.0)
+        nc.scalar.dma_start(out=b_rows[0:CHUNKS, :], in_=b.rearrange("(c p) o -> c (p o)", p=P))
+        ident = keep.tile([P, P], F32, name="ident")
+        make_identity(nc, ident[:])
+        b_turned = psum.tile([P, P], F32, name="b_turned")
+        nc.tensor.transpose(b_turned[:], b_rows[:], ident[:])
+        bias = keep.tile([P, CHUNKS], F32, name="bias")
+
+        w_g = keep.tile([P, 2, V], F32, name="w_g")
+        x_q = keep.tile([P, S, PACK], BF16, name="x_q", align_bytes=64)
+        w_q = keep.tile([P, V, PACK], BF16, name="w_q", align_bytes=64)
+        x_codes = keep.tile([P, S], U32, name="x_codes", align_bytes=64)
+        x_scales = keep.tile([P, S], U8, name="x_scales", align_bytes=64)
+        w_codes = keep.tile([P, V], U32, name="w_codes", align_bytes=64)
+        w_scales = keep.tile([P, V], U8, name="w_scales", align_bytes=64)
+
+        def interleave(dst, src, pair, cols):
+            nc.scalar.copy(
+                out=dst[:, cols, 2 * pair : 2 * pair + 2],
+                in_=src[:, :, cols].rearrange("p t c -> p c t"),
+            )
+
+        def quantise(codes, scales, src, cols):
+            nc.vector.quantize_mx(
+                out=codes[:, cols].bitcast(FP8X4),
+                scales=scales[:, cols],
+                in_=src[:, cols, :].rearrange("p c t -> p (c t)"),
+            )
+
+        every = slice(0, S)
+
+        w_half = [keep.tile([P, N], BF16, name=f"w_half{t}") for t in range(2)]
+
+        for t in (0, 1):
+            nc.vector.tensor_copy(x_q[:, :, t], x_raw[t][:].indirect(offs_t[:]))
+        nc.scalar.copy(out=w_half[0][:], in_=w_raw[0][:])
+        nc.scalar.activation(w_q[:, :, 0], w_half[0][:].indirect(pos1_t[:]), COPY)
+        for t in (2, 3):
+            nc.vector.tensor_copy(x_q[:, :, t], x_raw[t][:].indirect(offs_t[:]))
+        nc.scalar.copy(out=bias[:], in_=b_turned[:, 0:CHUNKS])
+        nc.vector.tensor_copy(w_half[1][:], w_raw[1][:])
+        nc.scalar.activation(w_q[:, :, 1], w_half[1][:].indirect(pos1_t[:]), COPY)
+        quantise(x_codes, x_scales, x_q, every)
+        nc.vector.tensor_copy(w_g[:, 0, :], w_raw[2][:].indirect(pos1_t[:]))
+
+        def gather_last(c):
+            cols = slice(CHUNK * c, CHUNK * (c + 1))
+            nc.vector.tensor_copy(
+                w_g[:, 1, cols],
+                w_raw[PACK - 1][:].indirect(pos1_t[:, CHUNK // 16 * c : CHUNK // 16 * (c + 1)]),
+            )
+            interleave(w_q, w_g, 1, cols)
+
+        def multiply(c):
+            cols = slice(CHUNK * c, CHUNK * (c + 1))
+            quantise(w_codes, w_scales, w_q, cols)
+            acc = psum.tile([P, S], F32, name=f"acc{c}")
+            nc.tensor.matmul_mx(
+                out=acc[:],
+                lhsT=w_codes[:, cols].bitcast(FP8X4),
+                lhsT_scale=w_scales[:, cols],
+                rhs=x_codes[:].bitcast(FP8X4),
+                rhs_scale=x_scales[:],
+                start=True,
+                stop=True,
+            )
+            return acc
+
+        def finish(c, acc):
+            result = keep.tile([P, S], F32, name=f"result{c}")
+            if c % 2 == 0:
+                nc.scalar.activation(result[:], acc[:], IDENTITY, bias=bias[:, c : c + 1])
+            else:
+                nc.vector.tensor_scalar(result[:], acc[:], bias[:, c : c + 1], None, op0=ADD)
+            nc.sync.dma_start(out=out[CHUNK * c : CHUNK * (c + 1), :], in_=result[:])
+
+        gather_last(0)
+        gather_last(1)
+        gather_last(2)
+        accs = [multiply(0)]
+        gather_last(3)
+        for c in range(1, CHUNKS):
+            accs.append(multiply(c))
+        for c in range(CHUNKS):
+            finish(c, accs[c])

@@ -36,15 +36,19 @@ def tile_picked_cross_bias_l_kernel(tc, xT, w, b, offs, pos1, out):
         x_raw = [keep.tile([P, T], F32, name=f"x_raw{t}") for t in range(PACK)]
         w_raw = [keep.tile([P, N], F32, name=f"w_raw{t}") for t in range(PACK)]
 
+        def load(tile, rows, t):
+            nc.sync.dma_start(out=tile[t][:], in_=rows[:, t, :])
+
         nc.sync.dma_start(out=offs_t[:], in_=offs)
-        nc.sync.dma_start(out=x_raw[0][:], in_=x_rows[:, 0, :])
-        nc.sync.dma_start(out=x_raw[1][:], in_=x_rows[:, 1, :])
+        load(x_raw, x_rows, 2)
+        load(x_raw, x_rows, 3)
+        load(x_raw, x_rows, 0)
         nc.sync.dma_start(out=pos1_t[:], in_=pos1)
-        nc.sync.dma_start(out=w_raw[0][:], in_=w_rows[:, 0, :])
-        nc.sync.dma_start(out=x_raw[2][:], in_=x_rows[:, 2, :])
-        nc.sync.dma_start(out=x_raw[3][:], in_=x_rows[:, 3, :])
-        for t in range(1, PACK):
-            nc.sync.dma_start(out=w_raw[t][:], in_=w_rows[:, t, :])
+        load(w_raw, w_rows, 0)
+        load(x_raw, x_rows, 1)
+        load(w_raw, w_rows, 1)
+        load(w_raw, w_rows, 2)
+        load(w_raw, w_rows, 3)
 
         b_rows = keep.tile([P, P], F32, name="b_rows")
         nc.vector.memset(b_rows[:], 0.0)
@@ -55,19 +59,12 @@ def tile_picked_cross_bias_l_kernel(tc, xT, w, b, offs, pos1, out):
         nc.tensor.transpose(b_turned[:], b_rows[:], ident[:])
         bias = keep.tile([P, CHUNKS], F32, name="bias")
 
-        w_g = keep.tile([P, 2, V], F32, name="w_g")
         x_q = keep.tile([P, S, PACK], BF16, name="x_q", align_bytes=64)
         w_q = keep.tile([P, V, PACK], BF16, name="w_q", align_bytes=64)
         x_codes = keep.tile([P, S], U32, name="x_codes", align_bytes=64)
         x_scales = keep.tile([P, S], U8, name="x_scales", align_bytes=64)
         w_codes = keep.tile([P, V], U32, name="w_codes", align_bytes=64)
         w_scales = keep.tile([P, V], U8, name="w_scales", align_bytes=64)
-
-        def interleave(dst, src, pair, cols):
-            nc.scalar.copy(
-                out=dst[:, cols, 2 * pair : 2 * pair + 2],
-                in_=src[:, :, cols].rearrange("p t c -> p c t"),
-            )
 
         def quantise(codes, scales, src, cols):
             nc.vector.quantize_mx(
@@ -78,57 +75,61 @@ def tile_picked_cross_bias_l_kernel(tc, xT, w, b, offs, pos1, out):
 
         every = slice(0, S)
 
-        w_half = [keep.tile([P, N], BF16, name=f"w_half{t}") for t in range(2)]
+        x_half = {t: keep.tile([P, T], BF16, name=f"x_half{t}") for t in (2, 3)}
+        w_half = {t: keep.tile([P, N], BF16, name=f"w_half{t}") for t in (0, 1)}
 
-        for t in (0, 1):
-            nc.vector.tensor_copy(x_q[:, :, t], x_raw[t][:].indirect(offs_t[:]))
-        nc.scalar.copy(out=w_half[0][:], in_=w_raw[0][:])
-        nc.scalar.activation(w_q[:, :, 0], w_half[0][:].indirect(pos1_t[:]), COPY)
-        for t in (2, 3):
-            nc.vector.tensor_copy(x_q[:, :, t], x_raw[t][:].indirect(offs_t[:]))
+        def scalar_gather(dst, half, offsets, t):
+            nc.scalar.activation(dst[:, :, t], half[t][:].indirect(offsets[:]), COPY)
+
+        def vector_gather(dst, raw, offsets, t):
+            nc.vector.tensor_copy(dst[:, :, t], raw[t][:].indirect(offsets[:]))
+
+        nc.vector.tensor_copy(x_half[2][:], x_raw[2][:])
+        scalar_gather(x_q, x_half, offs_t, 2)
+        nc.vector.tensor_copy(x_half[3][:], x_raw[3][:])
+        scalar_gather(x_q, x_half, offs_t, 3)
+        vector_gather(x_q, x_raw, offs_t, 0)
+        nc.vector.tensor_copy(w_half[0][:], w_raw[0][:])
+        scalar_gather(w_q, w_half, pos1_t, 0)
+        vector_gather(x_q, x_raw, offs_t, 1)
+        nc.scalar.copy(out=w_half[1][:], in_=w_raw[1][:])
+        scalar_gather(w_q, w_half, pos1_t, 1)
         nc.scalar.copy(out=bias[:], in_=b_turned[:, 0:CHUNKS])
-        nc.vector.tensor_copy(w_half[1][:], w_raw[1][:])
-        nc.scalar.activation(w_q[:, :, 1], w_half[1][:].indirect(pos1_t[:]), COPY)
         quantise(x_codes, x_scales, x_q, every)
-        nc.vector.tensor_copy(w_g[:, 0, :], w_raw[2][:].indirect(pos1_t[:]))
+        vector_gather(w_q, w_raw, pos1_t, 2)
 
-        def gather_last(c):
-            cols = slice(CHUNK * c, CHUNK * (c + 1))
-            nc.vector.tensor_copy(
-                w_g[:, 1, cols],
-                w_raw[PACK - 1][:].indirect(pos1_t[:, CHUNK // 16 * c : CHUNK // 16 * (c + 1)]),
-            )
-            interleave(w_q, w_g, 1, cols)
-
-        def multiply(c):
-            cols = slice(CHUNK * c, CHUNK * (c + 1))
-            quantise(w_codes, w_scales, w_q, cols)
-            acc = psum.tile([P, S], F32, name=f"acc{c}")
+        def multiply(c, j0, width):
+            acc = psum.tile([P, width], F32, name=f"acc{c}_{j0}")
+            rows, cols = slice(CHUNK * c, CHUNK * (c + 1)), slice(j0, j0 + width)
             nc.tensor.matmul_mx(
                 out=acc[:],
-                lhsT=w_codes[:, cols].bitcast(FP8X4),
-                lhsT_scale=w_scales[:, cols],
-                rhs=x_codes[:].bitcast(FP8X4),
-                rhs_scale=x_scales[:],
+                lhsT=w_codes[:, rows].bitcast(FP8X4),
+                lhsT_scale=w_scales[:, rows],
+                rhs=x_codes[:, cols].bitcast(FP8X4),
+                rhs_scale=x_scales[:, cols],
                 start=True,
                 stop=True,
             )
-            return acc
-
-        def finish(c, acc):
-            result = keep.tile([P, S], F32, name=f"result{c}")
-            if c % 2 == 0:
-                nc.scalar.activation(result[:], acc[:], IDENTITY, bias=bias[:, c : c + 1])
-            else:
+            result = keep.tile([P, width], F32, name=f"result{c}_{j0}")
+            if c == CHUNKS - 1 and j0 == 0:
                 nc.vector.tensor_scalar(result[:], acc[:], bias[:, c : c + 1], None, op0=ADD)
-            nc.sync.dma_start(out=out[CHUNK * c : CHUNK * (c + 1), :], in_=result[:])
+            else:
+                nc.scalar.activation(result[:], acc[:], IDENTITY, bias=bias[:, c : c + 1])
+            nc.sync.dma_start(out=out[rows, cols], in_=result[:])
+
+        def gather_last(c):
+            nc.vector.tensor_copy(
+                w_q[:, CHUNK * c : CHUNK * (c + 1), 3],
+                w_raw[3][:].indirect(pos1_t[:, CHUNK // 16 * c : CHUNK // 16 * (c + 1)]),
+            )
 
         gather_last(0)
-        gather_last(1)
-        gather_last(2)
-        accs = [multiply(0)]
-        gather_last(3)
-        for c in range(1, CHUNKS):
-            accs.append(multiply(c))
         for c in range(CHUNKS):
-            finish(c, accs[c])
+            if c < CHUNKS - 1:
+                gather_last(c + 1)
+            quantise(w_codes, w_scales, w_q, slice(CHUNK * c, CHUNK * (c + 1)))
+            if c < CHUNKS - 1:
+                multiply(c, 0, S)
+            else:
+                multiply(c, 0, S // 2)
+                multiply(c, S // 2, S // 2)

@@ -39,8 +39,8 @@ def tile_picked_cross_bias_l_kernel(tc, xT, w, b, offs, pos1, out):
         def load(tile, rows, t):
             nc.sync.dma_start(out=tile[t][:], in_=rows[:, t, :])
 
-        nc.sync.dma_start(out=offs_t[:], in_=offs)
         load(x_raw, x_rows, 2)
+        nc.sync.dma_start(out=offs_t[:], in_=offs)
         load(x_raw, x_rows, 3)
         load(x_raw, x_rows, 0)
         nc.sync.dma_start(out=pos1_t[:], in_=pos1)
@@ -49,6 +49,10 @@ def tile_picked_cross_bias_l_kernel(tc, xT, w, b, offs, pos1, out):
         load(w_raw, w_rows, 1)
         load(w_raw, w_rows, 2)
         load(w_raw, w_rows, 3)
+
+        warm = keep.tile([P, 2], F32, name="warm")
+        nc.vector.memset(warm[:], 0.0)
+        nc.scalar.activation(warm[:, 1:2], warm[:, 0:1], COPY)
 
         b_rows = keep.tile([P, P], F32, name="b_rows")
         nc.vector.memset(b_rows[:], 0.0)
@@ -59,6 +63,7 @@ def tile_picked_cross_bias_l_kernel(tc, xT, w, b, offs, pos1, out):
         nc.tensor.transpose(b_turned[:], b_rows[:], ident[:])
         bias = keep.tile([P, CHUNKS], F32, name="bias")
 
+        w_g = keep.tile([P, 2, V], F32, name="w_g")
         x_q = keep.tile([P, S, PACK], BF16, name="x_q", align_bytes=64)
         w_q = keep.tile([P, V, PACK], BF16, name="w_q", align_bytes=64)
         x_codes = keep.tile([P, S], U32, name="x_codes", align_bytes=64)
@@ -96,7 +101,7 @@ def tile_picked_cross_bias_l_kernel(tc, xT, w, b, offs, pos1, out):
         scalar_gather(w_q, w_half, pos1_t, 1)
         nc.scalar.copy(out=bias[:], in_=b_turned[:, 0:CHUNKS])
         quantise(x_codes, x_scales, x_q, every)
-        vector_gather(w_q, w_raw, pos1_t, 2)
+        nc.vector.tensor_copy(w_g[:, 0, :], w_raw[2][:].indirect(pos1_t[:]))
 
         def multiply(c, j0, width):
             acc = psum.tile([P, width], F32, name=f"acc{c}_{j0}")
@@ -111,7 +116,7 @@ def tile_picked_cross_bias_l_kernel(tc, xT, w, b, offs, pos1, out):
                 stop=True,
             )
             result = keep.tile([P, width], F32, name=f"result{c}_{j0}")
-            if c == CHUNKS - 1 and j0 == 0:
+            if (c, j0) in ((1, 0), (3, 0)):
                 nc.vector.tensor_scalar(result[:], acc[:], bias[:, c : c + 1], None, op0=ADD)
             else:
                 nc.scalar.activation(result[:], acc[:], IDENTITY, bias=bias[:, c : c + 1])
@@ -119,17 +124,32 @@ def tile_picked_cross_bias_l_kernel(tc, xT, w, b, offs, pos1, out):
 
         def gather_last(c):
             nc.vector.tensor_copy(
-                w_q[:, CHUNK * c : CHUNK * (c + 1), 3],
+                w_g[:, 1, CHUNK * c : CHUNK * (c + 1)],
                 w_raw[3][:].indirect(pos1_t[:, CHUNK // 16 * c : CHUNK // 16 * (c + 1)]),
             )
 
-        gather_last(0)
-        for c in range(CHUNKS):
-            if c < CHUNKS - 1:
-                gather_last(c + 1)
+        def interleave(c):
+            rows = slice(CHUNK * c, CHUNK * (c + 1))
+            copy = nc.vector.tensor_copy if c == 0 else nc.scalar.copy
+            copy(out=w_q[:, rows, 2:4], in_=w_g[:, :, rows].rearrange("p t c -> p c t"))
+
+        def quantise_words(c):
             quantise(w_codes, w_scales, w_q, slice(CHUNK * c, CHUNK * (c + 1)))
-            if c < CHUNKS - 1:
-                multiply(c, 0, S)
-            else:
-                multiply(c, 0, S // 2)
-                multiply(c, S // 2, S // 2)
+
+        gather_last(0)
+        gather_last(1)
+        interleave(0)
+        interleave(1)
+        gather_last(2)
+        interleave(2)
+        quantise_words(0)
+        gather_last(3)
+        interleave(3)
+        quantise_words(1)
+        quantise_words(2)
+        quantise_words(3)
+        multiply(0, 0, S)
+        multiply(1, 0, S)
+        multiply(2, 0, S)
+        multiply(3, 0, S // 2)
+        multiply(3, S // 2, S // 2)

from contextlib import ExitStack

import concourse.mybir as mybir
from concourse.masks import make_identity

F32 = mybir.dt.float32
BF16 = mybir.dt.bfloat16
U16 = mybir.dt.uint16
U32 = mybir.dt.uint32
U8 = mybir.dt.uint8
FP8X4 = mybir.dt.float8_e4m3fn_x4
COPY = mybir.ActivationFunctionType.Copy
IDENTITY = mybir.ActivationFunctionType.Identity
ADD = mybir.AluOpType.add

P = 128
PACK = 4
K, T, S, V, N = 512, 1024, 512, 512, 1024
CHUNK = 128
CHUNKS = V // CHUNK
FLOPS = 2 * K * S * V


def tile_picked_cross_bias_l_kernel(tc, xT, w, b, offs, pos1, out):
    nc = tc.nc
    with ExitStack() as ctx:
        lists = ctx.enter_context(tc.tile_pool(name="lists", bufs=1))
        keep = ctx.enter_context(tc.tile_pool(name="keep", bufs=1))
        psum = ctx.enter_context(tc.psum_pool(name="psum", bufs=1))

        offs_t = lists.tile([P, S // 16], U16, name="offs_t")
        pos1_t = lists.tile([P, V // 16], U16, name="pos1_t")

        x_rows = xT.rearrange("(p t) n -> p t n", t=PACK)
        w_rows = w.rearrange("(p t) n -> p t n", t=PACK)
        x_raw = [keep.tile([P, T], F32, name=f"x_raw{t}") for t in range(PACK)]
        w_raw = [keep.tile([P, N], F32, name=f"w_raw{t}") for t in range(PACK)]

        def load(tile, rows, t):
            nc.sync.dma_start(out=tile[t][:], in_=rows[:, t, :])

        load(x_raw, x_rows, 2)
        nc.sync.dma_start(out=offs_t[:], in_=offs)
        load(x_raw, x_rows, 3)
        load(x_raw, x_rows, 0)
        nc.sync.dma_start(out=pos1_t[:], in_=pos1)
        load(w_raw, w_rows, 0)
        load(x_raw, x_rows, 1)
        load(w_raw, w_rows, 1)
        load(w_raw, w_rows, 2)
        load(w_raw, w_rows, 3)

        warm = keep.tile([P, 2], F32, name="warm")
        nc.vector.memset(warm[:], 0.0)
        nc.scalar.activation(warm[:, 1:2], warm[:, 0:1], COPY)

        b_rows = keep.tile([P, P], F32, name="b_rows")
        nc.vector.memset(b_rows[:], 0.0)
        nc.scalar.dma_start(out=b_rows[0:CHUNKS, :], in_=b.rearrange("(c p) o -> c (p o)", p=P))
        ident = keep.tile([P, P], F32, name="ident")
        make_identity(nc, ident[:])
        b_turned = psum.tile([P, P], F32, name="b_turned")
        nc.tensor.transpose(b_turned[:], b_rows[:], ident[:])
        bias = keep.tile([P, CHUNKS], F32, name="bias")

        w_g = keep.tile([P, 2, V], F32, name="w_g")
        x_q = keep.tile([P, S, PACK], BF16, name="x_q", align_bytes=64)
        w_q = keep.tile([P, V, PACK], BF16, name="w_q", align_bytes=64)
        x_codes = keep.tile([P, S], U32, name="x_codes", align_bytes=64)
        x_scales = keep.tile([P, S], U8, name="x_scales", align_bytes=64)
        w_codes = keep.tile([P, V], U32, name="w_codes", align_bytes=64)
        w_scales = keep.tile([P, V], U8, name="w_scales", align_bytes=64)

        def quantise(codes, scales, src, cols):
            nc.vector.quantize_mx(
                out=codes[:, cols].bitcast(FP8X4),
                scales=scales[:, cols],
                in_=src[:, cols, :].rearrange("p c t -> p (c t)"),
            )

        every = slice(0, S)

        x_half = {t: keep.tile([P, T], BF16, name=f"x_half{t}") for t in (2, 3)}
        w_half = {t: keep.tile([P, N], BF16, name=f"w_half{t}") for t in (0, 1)}

        def scalar_gather(dst, half, offsets, t):
            nc.scalar.activation(dst[:, :, t], half[t][:].indirect(offsets[:]), COPY)

        def vector_gather(dst, raw, offsets, t):
            nc.vector.tensor_copy(dst[:, :, t], raw[t][:].indirect(offsets[:]))

        nc.vector.tensor_copy(x_half[2][:], x_raw[2][:])
        scalar_gather(x_q, x_half, offs_t, 2)
        nc.vector.tensor_copy(x_half[3][:], x_raw[3][:])
        scalar_gather(x_q, x_half, offs_t, 3)
        vector_gather(x_q, x_raw, offs_t, 0)
        nc.vector.tensor_copy(w_half[0][:], w_raw[0][:])
        scalar_gather(w_q, w_half, pos1_t, 0)
        vector_gather(x_q, x_raw, offs_t, 1)
        nc.scalar.copy(out=w_half[1][:], in_=w_raw[1][:])
        scalar_gather(w_q, w_half, pos1_t, 1)
        nc.scalar.copy(out=bias[:], in_=b_turned[:, 0:CHUNKS])
        quantise(x_codes, x_scales, x_q, every)
        nc.vector.tensor_copy(w_g[:, 0, :], w_raw[2][:].indirect(pos1_t[:]))

        def multiply(c, j0, width):
            acc = psum.tile([P, width], F32, name=f"acc{c}_{j0}")
            rows, cols = slice(CHUNK * c, CHUNK * (c + 1)), slice(j0, j0 + width)
            nc.tensor.matmul_mx(
                out=acc[:],
                lhsT=w_codes[:, rows].bitcast(FP8X4),
                lhsT_scale=w_scales[:, rows],
                rhs=x_codes[:, cols].bitcast(FP8X4),
                rhs_scale=x_scales[:, cols],
                start=True,
                stop=True,
            )
            result = keep.tile([P, width], F32, name=f"result{c}_{j0}")
            if (c, j0) in ((1, 0), (3, 0)):
                nc.vector.tensor_scalar(result[:], acc[:], bias[:, c : c + 1], None, op0=ADD)
            else:
                nc.scalar.activation(result[:], acc[:], IDENTITY, bias=bias[:, c : c + 1])
            nc.sync.dma_start(out=out[rows, cols], in_=result[:])

        def gather_last(c):
            nc.vector.tensor_copy(
                w_g[:, 1, CHUNK * c : CHUNK * (c + 1)],
                w_raw[3][:].indirect(pos1_t[:, CHUNK // 16 * c : CHUNK // 16 * (c + 1)]),
            )

        def interleave(c):
            rows = slice(CHUNK * c, CHUNK * (c + 1))
            copy = nc.vector.tensor_copy if c == 0 else nc.scalar.copy
            copy(out=w_q[:, rows, 2:4], in_=w_g[:, :, rows].rearrange("p t c -> p c t"))

        def quantise_words(c):
            quantise(w_codes, w_scales, w_q, slice(CHUNK * c, CHUNK * (c + 1)))

        gather_last(0)
        gather_last(1)
        interleave(0)
        interleave(1)
        gather_last(2)
        interleave(2)
        quantise_words(0)
        gather_last(3)
        interleave(3)
        quantise_words(1)
        quantise_words(2)
        quantise_words(3)
        multiply(0, 0, S)
        multiply(1, 0, S)
        multiply(2, 0, S)
        multiply(3, 0, S // 2)
        multiply(3, S // 2, S // 2)
